import numpy as np
import ml_dtypes


def mxq(x, axis, fmt="e4m3"):
    dtype, down = {"e4m3": (ml_dtypes.float8_e4m3fn, 7), "e5m2": (ml_dtypes.float8_e5m2, 14)}[fmt]
    v = np.moveaxis(np.asarray(x, np.float32).astype(ml_dtypes.bfloat16).astype(np.float64), axis, -1)
    blocks = v.reshape(v.shape[:-1] + (-1, 32))
    amax = np.abs(blocks).max(-1, keepdims=True)
    byte = np.maximum(np.where(amax > 0, np.frexp(amax)[1] - 1 + 127, 0) - down, 1)
    scale = np.exp2(byte - 127.0)
    codes = (blocks / scale).astype(np.float32).astype(dtype).astype(np.float64)
    return np.moveaxis((codes * scale).reshape(v.shape), -1, axis)


WIDE = False


def mx_kscale(k):
    if not WIDE:
        return np.ones(k)
    levels = np.array([10, -10, 5, -5, 0])
    if k % 512:
        return np.exp2(np.random.permutation(np.resize(levels, k // 32))).repeat(32)
    a = np.empty((k // 512, 16))
    for p in range(k // 512):
        a[p, :8] = np.random.permutation(np.resize(levels, 8))
        for g in range(8):
            far = levels[np.abs(levels - a[p, g]) >= 10]
            a[p, g + 8] = far[np.random.randint(len(far))]
    return np.exp2(a.ravel()).repeat(32)


BF16 = ml_dtypes.bfloat16


def bf(x):
    return np.asarray(x, np.float32).astype(BF16)


def f64(x):
    return np.asarray(x).astype(np.float64)


E2M1 = np.array([0.0, 0.5, 1.0, 1.5, 2.0, 3.0, 4.0, 6.0, -0.0, -0.5, -1.0, -1.5, -2.0, -3.0, -4.0, -6.0])


def pack_weight(w, fmt):
    k, n = w.shape
    w = f64(bf(w)).reshape(k // 32, 32, n)
    amax = np.abs(w).max(1)
    if fmt == "e4m3":
        byte = np.frexp(amax)[1] - 1 + 127 - 7
    else:
        mant, ex = np.frexp(amax / 6.0)
        byte = np.where(mant > 0.5, ex, ex - 1) + 127
    byte = np.clip(np.where(amax > 0, byte, 1), 1, 254)
    scaled = (w * np.exp2(127.0 - byte)[:, None, :]).reshape(k, n).astype(np.float32)
    by_word = np.ascontiguousarray(scaled.reshape(k // 512, 128, 4, n).transpose(0, 1, 3, 2))
    if fmt == "e4m3":
        words = by_word.astype(ml_dtypes.float8_e4m3fn).view(np.uint8)
    else:
        c = by_word.astype(ml_dtypes.float4_e2m1fn).view(np.uint8) & 0xF
        words = c[..., 0::2] | (c[..., 1::2] << 4)
    return np.ascontiguousarray(words), np.ascontiguousarray(byte.astype(np.uint8).reshape(k // 512, 16, n))


def unpack_weight(words, scales, fmt):
    g, p, n, _ = words.shape
    if fmt == "e4m3":
        vals = np.ascontiguousarray(words).view(ml_dtypes.float8_e4m3fn).astype(np.float64)
    else:
        nib = np.empty((g, p, n, 4), np.uint8)
        nib[..., 0::2] = words & 0xF
        nib[..., 1::2] = words >> 4
        vals = E2M1[nib]
    vals = vals * np.repeat(np.exp2(scales.astype(np.float64) - 127.0), 8, axis=1)[..., None]
    return vals.transpose(0, 1, 3, 2).reshape(g * 512, n)
def pack4(w):
    words, scales = pack_weight(w, "e2m1")
    return words.reshape(words.shape[0], 128, -1), scales


def unpack4(words, scales):
    return unpack_weight(words.reshape(words.shape[0], 128, -1, 2), scales, "e2m1")


def planes(Y):
    n, m = Y.shape
    b = f64(bf(Y)).reshape(n // 32, 32, m)
    amax = np.abs(b).max(1)
    byte = np.clip(np.where(amax > 0, np.frexp(amax)[1] - 1 + 127 - 7, 1), 1, 254)
    codes = (b * np.exp2(127.0 - byte)[:, None, :]).reshape(n, m).astype(np.float32).astype(ml_dtypes.float8_e4m3fn).view(np.uint8)
    words = codes.reshape(n // 512, 128, 4, m).transpose(0, 1, 3, 2)
    return np.ascontiguousarray(words), np.ascontiguousarray(byte.astype(np.uint8).reshape(n // 512, 16, m))


F, J, D, A, H, T = 1024, 1024, 1024, 512, 4, 512


def scale_heads(q, head_w):
    n_feat, n_cols = q.shape
    n_heads = head_w.shape[0]
    per_head = q.reshape(n_feat, n_heads, n_cols // n_heads)
    return (per_head * head_w[None, :, None]).reshape(n_feat, n_cols)


def setup_inputs():
    s, u = mx_kscale(D), mx_kscale(D)
    t = mx_kscale(A)
    r = mx_kscale(T)
    dq = bf(np.random.standard_normal((F, D)) * s)
    dk = bf(np.random.standard_normal((J, D)) * u)
    wq_words, wq_scales = pack4(np.random.standard_normal((D, A)) / np.sqrt(D) / s[:, None] * t)
    wk_words, wk_scales = pack4(np.random.standard_normal((D, A)) / np.sqrt(D) / u[:, None] / t)
    return {
        "dq": dq,
        "dk": dk,
        "wq_words": wq_words,
        "wq_scales": wq_scales,
        "wk_words": wk_words,
        "wk_scales": wk_scales,
        "head_w": bf(1.0 + 0.25 * np.random.standard_normal(H)),
        "aq": bf(np.random.standard_normal((T, F)) * T**0.25 * r[:, None]),
        "ak": bf(np.random.standard_normal((T, J)) * T**0.25 / r[:, None]),
        "g": bf(np.random.standard_normal(T)),
    }


def core(dq, dk, wq_words, wq_scales, wk_words, wk_scales, head_w, aq, ak, g):
    n_pairs = aq.shape[0]
    head_dim = wq_scales.shape[2] // head_w.shape[0]

    q = mxq(f64(dq), 1, "e4m3") @ unpack4(wq_words, wq_scales)
    k = mxq(f64(dk), 1, "e4m3") @ unpack4(wk_words, wk_scales)

    qw = scale_heads(q, f64(head_w))

    m = (mxq(qw, 1, "e4m3") @ mxq(k.T, 0, "e4m3")) / np.sqrt(head_dim)

    c = (mxq(f64(aq).T, 1, "e4m3") @ mxq(f64(g)[:, None] * f64(ak), 0, "e4m3")) / n_pairs

    return m * c


def reference(dq, dk, wq_words, wq_scales, wk_words, wk_scales, head_w, aq, ak, g):
    R_out = core(dq, dk, wq_words, wq_scales, wk_words, wk_scales, head_w, aq, ak, g)
    words, scales = planes(R_out.T)
    return R_out, words, scales

@@ -1,0 +1,404 @@
+import math
+from contextlib import ExitStack
+
+import concourse.mybir as mybir
+from concourse.masks import make_identity
+
+F, J, D, A, H, T = 1024, 1024, 1024, 512, 4, 512
+FLOPS = 2 * F * D * A + 2 * J * D * A + 2 * F * J * A + 2 * F * J * T
+
+F32 = mybir.dt.float32
+BF16 = mybir.dt.bfloat16
+I32 = mybir.dt.int32
+U32 = mybir.dt.uint32
+U8 = mybir.dt.uint8
+FP8X4 = mybir.dt.float8_e4m3fn_x4
+FP4X4 = mybir.dt.float4_e2m1fn_x4
+COPY = mybir.ActivationFunctionType.Copy
+MULT = mybir.AluOpType.mult
+
+P = 128
+HALF = 512
+PAIR = 256
+BANKS = 8
+OUT_FACTOR = 1.0 / (math.sqrt(A // H) * T)
+
+
+def tile_featurepairqkscoreattribution_x2_kernel(
+    tc, dq, dk, wq_words, wq_scales, wk_words, wk_scales, head_w, aq, ak, g, out_0, out_1, out_2
+):
+    nc = tc.nc
+    with ExitStack() as ctx:
+        keep = ctx.enter_context(tc.tile_pool(name="keep", bufs=1))
+        flow = ctx.enter_context(tc.tile_pool(name="flow", bufs=3))
+        psum = ctx.enter_context(tc.psum_pool(name="psum", bufs=1))
+        ctx.enter_context(tc.manual_schedule())
+
+        banks_taken = []
+
+        def next_bank():
+            n = len(banks_taken)
+            banks_taken.append(n)
+            return psum.tile([P, HALF], F32, name="bank%d" % n, tag="bank%d" % (n % BANKS))
+
+        def operand(name, width):
+            codes = keep.tile([P, width], U32, name=name + "_codes", align_bytes=256)
+            scales = keep.tile([P, width], U8, name=name + "_scales", align_bytes=256)
+            return codes, scales
+
+        def quantize(target, cols, values):
+            codes, scales = target
+            nc.vector.quantize_mx(out=codes[:, cols].bitcast(FP8X4), scales=scales[:, cols], in_=values)
+
+        ident = keep.tile([P, P], F32, name="ident")
+        make_identity(nc, ident[:])
+
+        head_row = keep.tile([P, H], BF16, name="head_row")
+        nc.scalar.dma_start(out=head_row[:], in_=head_w.partition_broadcast(P))
+        g_rows = keep.tile([P, 4], BF16, name="g_rows")
+        head_col = keep.tile([P, 1], F32, name="head_col")
+        for h in range(H):
+            rows = slice(32 * h, 32 * h + 32)
+            nc.scalar.activation(out=head_col[rows, :], in_=head_row[rows, h : h + 1], func=COPY)
+
+        warm_in = keep.tile([P, 4 * PAIR], BF16, name="warm_in", align_bytes=64)
+        nc.vector.memset(warm_in[:].bitcast(I32), 0)
+        raw_scales = {}
+        for side in ("k", "q"):
+            raw_scales[side] = keep.tile([P, 2, A], U8, name="raw_scales_" + side, align_bytes=64)
+            nc.vector.memset(raw_scales[side][:].bitcast(I32), 0)
+            if side == "k":
+                warm_mx = operand("warm", PAIR)
+                quantize(warm_mx, slice(0, PAIR), warm_in[:])
+
+        directions = {}
+        raw_words = {}
+        tokens = {}
+
+        def load_directions(side, n):
+            src = dq if side == "q" else dk
+            pair = keep.tile([P, 2, D], BF16, name="dir_%s%d" % (side, n), align_bytes=64)
+            nc.sync.dma_start(out=pair[:], in_=src[PAIR * n : PAIR * (n + 1), :].rearrange("(s p) d -> p s d", p=P))
+            for s in range(2):
+                directions[side, n, s] = pair[:, s, :]
+
+        def load_directions_singly(side, n):
+            src = dq if side == "q" else dk
+            for s in range(2):
+                single = keep.tile([P, D], BF16, name="dir_%s%d_%d" % (side, n, s), align_bytes=64)
+                nc.sync.dma_start(out=single[:], in_=src[PAIR * n + P * s : PAIR * n + P * (s + 1), :])
+                directions[side, n, s] = single[:]
+
+        def load_words(side):
+            src = wq_words if side == "q" else wk_words
+            raw_words[side] = keep.tile([P, 2, 2 * A], U8, name="raw_words_" + side, align_bytes=64)
+            nc.sync.dma_start(out=raw_words[side][:].bitcast(I32), in_=src.rearrange("g p n -> p g n").bitcast(I32))
+
+        def load_scales(side, quadrants):
+            src = wq_scales if side == "q" else wk_scales
+            for quad in quadrants:
+                nc.sync.dma_start(
+                    out=raw_scales[side][32 * quad : 32 * quad + 4, :, :].bitcast(I32),
+                    in_=src[:, 4 * quad : 4 * quad + 4, :].rearrange("g r n -> r g n").bitcast(I32),
+                )
+
+        def load_tokens(side, half):
+            src = aq if side == "q" else ak
+            tokens[side, half] = keep.tile([P, 4, HALF], BF16, name="tok_%s%d" % (side, half), align_bytes=64)
+            nc.sync.dma_start(out=tokens[side, half][:], in_=src[:, HALF * half : HALF * (half + 1)].rearrange("(p t) n -> p t n", t=4))
+
+        load_directions_singly("k", 0)
+        load_words("k")
+        load_scales("k", range(4))
+        load_directions("k", 1)
+        load_tokens("k", 0)
+        nc.sync.dma_start(out=g_rows[:], in_=g.rearrange("(p t) -> p t", t=4))
+        load_tokens("q", 0)
+        load_directions("q", 0)
+        load_words("q")
+        load_scales("q", range(4))
+        load_directions("q", 1)
+        load_tokens("k", 1)
+        load_directions("k", 2)
+        load_tokens("q", 1)
+        load_directions("k", 3)
+        load_directions("q", 2)
+        load_directions("q", 3)
+
+        weights = {}
+
+        def sort_weight(side):
+            words = keep.tile([P, 2, 2 * A], U8, name="words_" + side, align_bytes=256)
+            scales = keep.tile([P, 2, A], U8, name="scales_" + side, align_bytes=256)
+            for target, source in ((words, raw_words[side]), (scales, raw_scales[side])):
+                nc.vector.tensor_copy(
+                    out=target[:].bitcast(I32).rearrange("p g (t b w) -> p g t b w", t=4, b=16),
+                    in_=source[:].bitcast(I32).rearrange("p g (b t w) -> p g t b w", t=4, b=16),
+                )
+            weights[side] = (words, scales)
+
+        turned = {}
+        dir_mx = {}
+        projected = {}
+        proj_mx = {("k", half): operand("k%d" % half, HALF) for half in range(2)}
+        for n in range(4):
+            proj_mx["q", n] = operand("q%d" % n, PAIR)
+        tok_mx = {(side, half): operand("a%s%d" % (side, half), HALF) for side in ("q", "k") for half in range(2)}
+        tok_grouped = {}
+        coact = {}
+        results = {}
+        rounded = {}
+        plane_in = {}
+        plane_codes = keep.tile([P, 2, F], U32, name="plane_codes", align_bytes=256)
+        plane_scales = keep.tile([P, F], U8, name="plane_scales", align_bytes=256)
+
+        def warm(count):
+            bank = next_bank()
+            for rep in range(count):
+                product(bank[:, 0:PAIR], warm_mx, 0, warm_mx)
+
+        def evac(engine, out, in_):
+            if engine == "vector":
+                nc.vector.tensor_copy(out=out, in_=in_)
+            else:
+                nc.scalar.copy(out=out, in_=in_)
+
+        def turn(side, n, engines=("scalar", "scalar")):
+            turned[side, n] = flow.tile([P, 2 * D], BF16, name="turned_%s%d" % (side, n), tag="turned", align_bytes=64)
+            for s in range(2):
+                words = directions[side, n, s].bitcast(F32)
+                bank = next_bank()
+                for gu in range(4):
+                    first = 256 * (gu // 2) + gu % 2
+                    nc.tensor.transpose(bank[:, P * gu : P * (gu + 1)], words[:, first : 256 * (gu // 2 + 1) : 2], ident[:])
+                evac(
+                    engines[s],
+                    turned[side, n][:, D * s : D * (s + 1)].bitcast(F32).rearrange("p (g f u) -> p g f u", g=2, u=2),
+                    bank[:].rearrange("p (g u f) -> p g f u", g=2, u=2),
+                )
+
+        def quantize_turned(side, n, split=False):
+            codes = flow.tile([P, HALF], U32, name="dir_codes_%s%d" % (side, n), tag="dir_codes", align_bytes=256)
+            scales = flow.tile([P, HALF], U8, name="dir_scales_%s%d" % (side, n), tag="dir_scales", align_bytes=256)
+            dir_mx[side, n] = (codes, scales)
+            if split:
+                for s in range(2):
+                    quantize(dir_mx[side, n], slice(PAIR * s, PAIR * (s + 1)), turned[side, n][:, D * s : D * (s + 1)])
+            else:
+                quantize(dir_mx[side, n], slice(0, HALF), turned[side, n][:])
+
+        def project(side, n):
+            words, wscales = weights[side]
+            codes, scales = dir_mx[side, n]
+            projected[side, n] = flow.tile([P, 4 * PAIR], BF16, name="proj_%s%d" % (side, n), tag="proj", align_bytes=64)
+            for s in range(2):
+                bank = next_bank()
+                for t in range(4):
+                    for grp in range(2):
+                        cols = slice(P * (2 * s + grp), P * (2 * s + grp + 1))
+                        nc.tensor.matmul_mx(
+                            out=bank[:, P * t : P * (t + 1)],
+                            lhsT=words[:, grp, 2 * P * t : 2 * P * (t + 1)].bitcast(FP4X4),
+                            lhsT_scale=wscales[:, grp, P * t : P * (t + 1)],
+                            rhs=codes[:, cols].bitcast(FP8X4),
+                            rhs_scale=scales[:, cols],
+                            start=(grp == 0),
+                            stop=(grp == 1),
+                        )
+                target = projected[side, n][:, HALF * s : HALF * (s + 1)].rearrange("p (f t) -> p f t", t=4)
+                source = bank[:].rearrange("p (t f) -> p f t", t=4)
+                if side == "q":
+                    nc.scalar.activation(out=target, in_=source, func=COPY, scale=head_col[:])
+                else:
+                    nc.scalar.copy(out=target, in_=source)
+
+        def quantize_projected(side, n, split=False):
+            if split:
+                for s in range(2):
+                    quantize(proj_mx["q", n], slice(P * s, P * (s + 1)), projected[side, n][:, HALF * s : HALF * (s + 1)])
+            elif side == "q":
+                quantize(proj_mx["q", n], slice(0, PAIR), projected[side, n][:])
+            else:
+                quantize(proj_mx["k", n // 2], slice(PAIR * (n % 2), PAIR * (n % 2 + 1)), projected[side, n][:])
+
+        def weigh_tokens(half):
+            weighed = flow.tile([P, 4, HALF], BF16, name="weighed%d" % half, tag="weighed", align_bytes=64)
+            for t in range(4):
+                nc.vector.tensor_scalar(out=weighed[:, t, :], in0=tokens["k", half][:, t, :], scalar1=g_rows[:, t : t + 1], scalar2=None, op0=MULT)
+            tokens["k", half] = weighed
+
+        def group_tokens(side, half):
+            tok_grouped[side, half] = flow.tile([P, 4 * HALF], BF16, name="grouped_%s%d" % (side, half), tag="grouped", align_bytes=64)
+            nc.vector.tensor_copy(
+                out=tok_grouped[side, half][:].rearrange("p (c i t) -> p c t i", i=4, t=4),
+                in_=tokens[side, half][:].rearrange("p t (c i) -> p c t i", i=4),
+            )
+
+        def quantize_tokens(side, half):
+            quantize(tok_mx[side, half], slice(0, HALF), tok_grouped[side, half][:])
+
+        def product(bank, stationary, first, moving):
+            cols = slice(first, first + P)
+            nc.tensor.matmul_mx(
+                out=bank[:],
+                lhsT=stationary[0][:, cols].bitcast(FP8X4),
+                lhsT_scale=stationary[1][:, cols],
+                rhs=moving[0][:].bitcast(FP8X4),
+                rhs_scale=moving[1][:],
+                start=True,
+                stop=True,
+            )
+
+        def coactivate(n, half):
+            coact[n, half] = flow.tile([P, 2, HALF], F32, name="coact%d_%d" % (n, half), tag="coact", bufs=5)
+            for s in range(2):
+                bank = next_bank()
+                product(bank, tok_mx["q", n // 2], PAIR * (n % 2) + P * s, tok_mx["k", half])
+                nc.scalar.copy(out=coact[n, half][:, s, :], in_=bank[:])
+
+        def score(n, half):
+            results[n, half] = flow.tile([P, 2, HALF], F32, name="result%d_%d" % (n, half), tag="result", bufs=4)
+            for s in range(2):
+                bank = next_bank()
+                product(bank, proj_mx["q", n], P * s, proj_mx["k", half])
+                nc.vector.scalar_tensor_tensor(
+                    out=results[n, half][:, s, :], in0=bank[:], scalar=OUT_FACTOR, in1=coact[n, half][:, s, :], op0=MULT, op1=MULT
+                )
+            nc.sync.dma_start(
+                out=out_0[PAIR * n : PAIR * (n + 1), HALF * half : HALF * (half + 1)].rearrange("(s p) j -> p s j", p=P),
+                in_=results[n, half][:],
+            )
+
+        def round_result(n, half, engines=("vector", "vector")):
+            rounded[n, half] = flow.tile([P, 2 * HALF], BF16, name="rounded%d_%d" % (n, half), tag="rounded", align_bytes=64)
+            if engines[0] == engines[1]:
+                evac(
+                    engines[0],
+                    rounded[n, half][:].rearrange("f (s u p e) -> f s u p e", s=2, u=2, e=2),
+                    results[n, half][:].rearrange("f s (p u e) -> f s u p e", u=2, e=2),
+                )
+            else:
+                for s in range(2):
+                    evac(
+                        engines[s],
+                        rounded[n, half][:, HALF * s : HALF * (s + 1)].rearrange("f (u p e) -> f u p e", u=2, e=2),
+                        results[n, half][:, s, :].rearrange("f (p u e) -> f u p e", u=2, e=2),
+                    )
+
+        def turn_result(n, half):
+            words = rounded[n, half][:].bitcast(F32)
+            bank = next_bank()
+            for su in range(4):
+                nc.tensor.transpose(bank[:, P * su : P * (su + 1)], words[:, P * su : P * (su + 1)], ident[:])
+            plane_in[n, half] = flow.tile([P, 4 * PAIR], BF16, name="plane_in%d_%d" % (n, half), tag="plane_in", bufs=4, align_bytes=64)
+            nc.scalar.copy(
+                out=plane_in[n, half][:].bitcast(F32).rearrange("p (s f u) -> p s f u", s=2, u=2),
+                in_=bank[:].rearrange("p (s u f) -> p s f u", s=2, u=2),
+            )
+
+        def quantize_result(n, half):
+            cols = slice(PAIR * n, PAIR * (n + 1))
+            nc.vector.quantize_mx(
+                out=plane_codes[:, half, cols].bitcast(FP8X4),
+                scales=plane_scales[4 * half : P, cols],
+                in_=plane_in[n, half][:],
+            )
+            nc.sync.dma_start(
+                out=out_1[half, :, cols, :].rearrange("p f t -> p (f t)").bitcast(I32),
+                in_=plane_codes[:, half, cols].bitcast(I32),
+            )
+
+        def store_scales():
+            for quad in range(4):
+                nc.sync.dma_start(
+                    out=out_2[:, 4 * quad : 4 * quad + 4, :].bitcast(I32),
+                    in_=plane_scales[32 * quad : 32 * quad + 8, :].bitcast(I32),
+                )
+
+        warm(6)
+        turn("k", 0)
+        warm(4)
+        sort_weight("k")
+        quantize_turned("k", 0, True)
+        turn("k", 1)
+        project("k", 0)
+        weigh_tokens(0)
+        quantize_turned("k", 1)
+        group_tokens("k", 0)
+        turn("q", 0)
+        quantize_projected("k", 0)
+        project("k", 1)
+        quantize_tokens("k", 0)
+        group_tokens("q", 0)
+        quantize_turned("q", 0)
+        sort_weight("q")
+        quantize_tokens("q", 0)
+        turn("q", 1)
+        quantize_projected("k", 1)
+        project("q", 0)
+        coactivate(0, 0)
+        weigh_tokens(1)
+        quantize_turned("q", 1)
+        group_tokens("k", 1)
+        turn("k", 2)
+        quantize_projected("q", 0)
+        project("q", 1)
+        score(0, 0)
+        coactivate(1, 0)
+        quantize_turned("k", 2)
+        quantize_tokens("k", 1)
+        turn("k", 3)
+        quantize_projected("q", 1)
+        round_result(0, 0)
+        project("k", 2)
+        score(1, 0)
+        coactivate(0, 1)
+        quantize_turned("k", 3)
+        turn("q", 2)
+        turn_result(0, 0)
+        quantize_projected("k", 2)
+        round_result(1, 0)
+        group_tokens("q", 1)
+        project("k", 3)
+        coactivate(1, 1)
+        quantize_turned("q", 2)
+        quantize_tokens("q", 1)
+        turn("q", 3)
+        turn_result(1, 0)
+        quantize_projected("k", 3)
+        quantize_result(0, 0)
+        project("q", 2)
+        score(0, 1)
+        quantize_turned("q", 3)
+        score(1, 1)
+        coactivate(2, 0)
+        quantize_projected("q", 2)
+        project("q", 3)
+        round_result(0, 1)
+        score(2, 0)
+        coactivate(2, 1)
+        quantize_result(1, 0)
+        round_result(1, 1)
+        quantize_projected("q", 3)
+        score(2, 1)
+        coactivate(3, 0)
+        turn_result(0, 1)
+        turn_result(1, 1)
+        round_result(2, 0)
+        score(3, 0)
+        coactivate(3, 1)
+        round_result(2, 1)
+        score(3, 1)
+        quantize_result(0, 1)
+        turn_result(2, 0)
+        round_result(3, 0, ("scalar", "scalar"))
+        quantize_result(1, 1)
+        turn_result(2, 1)
+        round_result(3, 1)
+        turn_result(3, 0)
+        quantize_result(2, 0)
+        turn_result(3, 1)
+        quantize_result(2, 1)
+        quantize_result(3, 0)
+        quantize_result(3, 1)
+        store_scales()

@@ -50,8 +50,6 @@ def tile_featurepairqkscoreattribution_x2_kernel(
             codes, scales = target
             nc.vector.quantize_mx(out=codes[:, cols].bitcast(FP8X4), scales=scales[:, cols], in_=values)
 
-        ident = keep.tile([P, P], F32, name="ident")
-        make_identity(nc, ident[:])
 
         head_row = keep.tile([P, H], BF16, name="head_row")
         nc.scalar.dma_start(out=head_row[:], in_=head_w.partition_broadcast(P))
@@ -70,6 +68,9 @@ def tile_featurepairqkscoreattribution_x2_kernel(
             if side == "k":
                 warm_mx = operand("warm", PAIR)
                 quantize(warm_mx, slice(0, PAIR), warm_in[:])
+
+        ident = keep.tile([P, P], F32, name="ident")
+        make_identity(nc, ident[:])
 
         directions = {}
         raw_words = {}
@@ -108,15 +109,15 @@ def tile_featurepairqkscoreattribution_x2_kernel(
             nc.sync.dma_start(out=tokens[side, half][:], in_=src[:, HALF * half : HALF * (half + 1)].rearrange("(p t) n -> p t n", t=4))
 
         load_directions_singly("k", 0)
+        load_directions("k", 1)
         load_words("k")
         load_scales("k", range(4))
-        load_directions("k", 1)
         load_tokens("k", 0)
         nc.sync.dma_start(out=g_rows[:], in_=g.rearrange("(p t) -> p t", t=4))
-        load_tokens("q", 0)
         load_directions("q", 0)
         load_words("q")
         load_scales("q", range(4))
+        load_tokens("q", 0)
         load_directions("q", 1)
         load_tokens("k", 1)
         load_directions("k", 2)
@@ -160,6 +161,8 @@ def tile_featurepairqkscoreattribution_x2_kernel(
         def evac(engine, out, in_):
             if engine == "vector":
                 nc.vector.tensor_copy(out=out, in_=in_)
+            elif engine == "gpsimd":
+                nc.gpsimd.tensor_scalar(out=out, in0=in_, scalar1=1.0, scalar2=1.0, op0=MULT, op1=MULT)
             else:
                 nc.scalar.copy(out=out, in_=in_)
 
@@ -249,12 +252,12 @@ def tile_featurepairqkscoreattribution_x2_kernel(
                 stop=True,
             )
 
-        def coactivate(n, half):
+        def coactivate(n, half, engines=("scalar", "scalar")):
             coact[n, half] = flow.tile([P, 2, HALF], F32, name="coact%d_%d" % (n, half), tag="coact", bufs=5)
             for s in range(2):
                 bank = next_bank()
                 product(bank, tok_mx["q", n // 2], PAIR * (n % 2) + P * s, tok_mx["k", half])
-                nc.scalar.copy(out=coact[n, half][:, s, :], in_=bank[:])
+                evac(engines[s], coact[n, half][:, s, :], bank[:])
 
         def score(n, half):
             results[n, half] = flow.tile([P, 2, HALF], F32, name="result%d_%d" % (n, half), tag="result", bufs=4)
@@ -270,8 +273,8 @@ def tile_featurepairqkscoreattribution_x2_kernel(
             )
 
         def round_result(n, half, engines=("vector", "vector")):
-            rounded[n, half] = flow.tile([P, 2 * HALF], BF16, name="rounded%d_%d" % (n, half), tag="rounded", align_bytes=64)
-            if engines[0] == engines[1]:
+            rounded[n, half] = flow.tile([P, 2 * HALF], BF16, name="rounded%d_%d" % (n, half), tag="rounded", bufs=4, align_bytes=64)
+            if engines == ("vector", "vector"):
                 evac(
                     engines[0],
                     rounded[n, half][:].rearrange("f (s u p e) -> f s u p e", s=2, u=2, e=2),
@@ -285,15 +288,16 @@ def tile_featurepairqkscoreattribution_x2_kernel(
                         results[n, half][:, s, :].rearrange("f (p u e) -> f u p e", u=2, e=2),
                     )
 
-        def turn_result(n, half):
+        def turn_result(n, half, engine="scalar"):
             words = rounded[n, half][:].bitcast(F32)
             bank = next_bank()
             for su in range(4):
                 nc.tensor.transpose(bank[:, P * su : P * (su + 1)], words[:, P * su : P * (su + 1)], ident[:])
-            plane_in[n, half] = flow.tile([P, 4 * PAIR], BF16, name="plane_in%d_%d" % (n, half), tag="plane_in", bufs=4, align_bytes=64)
-            nc.scalar.copy(
-                out=plane_in[n, half][:].bitcast(F32).rearrange("p (s f u) -> p s f u", s=2, u=2),
-                in_=bank[:].rearrange("p (s u f) -> p s f u", s=2, u=2),
+            plane_in[n, half] = flow.tile([P, 4 * PAIR], BF16, name="plane_in%d_%d" % (n, half), tag="plane_in", bufs=7, align_bytes=64)
+            evac(
+                engine,
+                plane_in[n, half][:].bitcast(F32).rearrange("p (s f u) -> p s f u", s=2, u=2),
+                bank[:].rearrange("p (s u f) -> p s f u", s=2, u=2),
             )
 
         def quantize_result(n, half):
@@ -310,95 +314,100 @@ def tile_featurepairqkscoreattribution_x2_kernel(
 
         def store_scales():
             for quad in range(4):
-                nc.sync.dma_start(
+                nc.scalar.dma_start(
                     out=out_2[:, 4 * quad : 4 * quad + 4, :].bitcast(I32),
                     in_=plane_scales[32 * quad : 32 * quad + 8, :].bitcast(I32),
                 )
 
-        warm(6)
-        turn("k", 0)
+        SV = ("scalar", "vector")
+        VS = ("vector", "scalar")
+        SS = ("scalar", "scalar")
+        VV = ("vector", "vector")
+        warm(5)
+        turn("k", 0, SV)
         warm(4)
-        sort_weight("k")
         quantize_turned("k", 0, True)
+        sort_weight("k")
         turn("k", 1)
         project("k", 0)
         weigh_tokens(0)
         quantize_turned("k", 1)
         group_tokens("k", 0)
         turn("q", 0)
-        quantize_projected("k", 0)
         project("k", 1)
-        quantize_tokens("k", 0)
-        group_tokens("q", 0)
-        quantize_turned("q", 0)
         sort_weight("q")
-        quantize_tokens("q", 0)
+        quantize_tokens("k", 0)
+        quantize_turned("q", 0)
+        group_tokens("q", 0)
+        quantize_projected("k", 0)
         turn("q", 1)
-        quantize_projected("k", 1)
         project("q", 0)
+        quantize_tokens("q", 0)
+        quantize_projected("k", 1)
+        quantize_turned("q", 1)
         coactivate(0, 0)
         weigh_tokens(1)
-        quantize_turned("q", 1)
+        quantize_projected("q", 0)
         group_tokens("k", 1)
         turn("k", 2)
-        quantize_projected("q", 0)
-        project("q", 1)
         score(0, 0)
+        project("q", 1)
         coactivate(1, 0)
         quantize_turned("k", 2)
         quantize_tokens("k", 1)
-        turn("k", 3)
         quantize_projected("q", 1)
-        round_result(0, 0)
-        project("k", 2)
-        score(1, 0)
-        coactivate(0, 1)
-        quantize_turned("k", 3)
-        turn("q", 2)
-        turn_result(0, 0)
-        quantize_projected("k", 2)
-        round_result(1, 0)
         group_tokens("q", 1)
-        project("k", 3)
+        turn("k", 3)
+        score(1, 0)
+        project("k", 2)
+        coactivate(0, 1)
         coactivate(1, 1)
-        quantize_turned("q", 2)
+        quantize_turned("k", 3)
+        round_result(0, 0)
         quantize_tokens("q", 1)
-        turn("q", 3)
+        round_result(1, 0)
+        turn("q", 2, VV)
+        turn("q", 3, SV)
+        turn_result(0, 0)
         turn_result(1, 0)
-        quantize_projected("k", 3)
+        quantize_projected("k", 2)
+        quantize_turned("q", 2)
+        project("k", 3)
+        quantize_turned("q", 3)
         quantize_result(0, 0)
         project("q", 2)
-        score(0, 1)
-        quantize_turned("q", 3)
-        score(1, 1)
-        coactivate(2, 0)
-        quantize_projected("q", 2)
-        project("q", 3)
-        round_result(0, 1)
-        score(2, 0)
-        coactivate(2, 1)
+        quantize_projected("k", 3)
         quantize_result(1, 0)
+        coactivate(2, 0, VS)
+        score(0, 1)
+        coactivate(2, 1)
+        quantize_projected("q", 2)
+        score(1, 1)
+        round_result(0, 1, SV)
+        project("q", 3)
+        score(2, 0)
+        coactivate(3, 0)
         round_result(1, 1)
         quantize_projected("q", 3)
         score(2, 1)
-        coactivate(3, 0)
+        coactivate(3, 1)
+        round_result(2, 0, SS)
         turn_result(0, 1)
         turn_result(1, 1)
-        round_result(2, 0)
+        round_result(2, 1, SV)
         score(3, 0)
-        coactivate(3, 1)
-        round_result(2, 1)
         score(3, 1)
-        quantize_result(0, 1)
+        round_result(3, 0, SV)
         turn_result(2, 0)
-        round_result(3, 0, ("scalar", "scalar"))
-        quantize_result(1, 1)
+        warm(5)
         turn_result(2, 1)
-        round_result(3, 1)
+        round_result(3, 1, ("vector", "vector", "split"))
+        quantize_result(0, 1)
         turn_result(3, 0)
-        quantize_result(2, 0)
+        quantize_result(1, 1)
         turn_result(3, 1)
-        quantize_result(2, 1)
+        quantize_result(2, 0)
         quantize_result(3, 0)
+        quantize_result(2, 1)
         quantize_result(3, 1)
         store_scales()

@@ -60,7 +60,7 @@ def tile_featurepairqkscoreattribution_x2_kernel(
             nc.scalar.activation(out=head_col[rows, :], in_=head_row[rows, h : h + 1], func=COPY)
 
         warm_in = keep.tile([P, 4 * PAIR], BF16, name="warm_in", align_bytes=64)
-        nc.vector.memset(warm_in[:].bitcast(I32), 0)
+        nc.gpsimd.memset(warm_in[:].bitcast(I32), 0)
         raw_scales = {}
         for side in ("k", "q"):
             raw_scales[side] = keep.tile([P, 2, A], U8, name="raw_scales_" + side, align_bytes=64)
@@ -109,20 +109,20 @@ def tile_featurepairqkscoreattribution_x2_kernel(
             nc.sync.dma_start(out=tokens[side, half][:], in_=src[:, HALF * half : HALF * (half + 1)].rearrange("(p t) n -> p t n", t=4))
 
         load_directions_singly("k", 0)
-        load_directions("k", 1)
-        load_words("k")
         load_scales("k", range(4))
-        load_tokens("k", 0)
+        load_words("k")
+        load_directions("k", 1)
         nc.sync.dma_start(out=g_rows[:], in_=g.rearrange("(p t) -> p t", t=4))
+        load_tokens("k", 0)
         load_directions("q", 0)
         load_words("q")
         load_scales("q", range(4))
         load_tokens("q", 0)
-        load_directions("q", 1)
-        load_tokens("k", 1)
         load_directions("k", 2)
-        load_tokens("q", 1)
+        load_tokens("k", 1)
         load_directions("k", 3)
+        load_tokens("q", 1)
+        load_directions("q", 1)
         load_directions("q", 2)
         load_directions("q", 3)
 
@@ -273,7 +273,7 @@ def tile_featurepairqkscoreattribution_x2_kernel(
             )
 
         def round_result(n, half, engines=("vector", "vector")):
-            rounded[n, half] = flow.tile([P, 2 * HALF], BF16, name="rounded%d_%d" % (n, half), tag="rounded", bufs=4, align_bytes=64)
+            rounded[n, half] = flow.tile([P, 2 * HALF], BF16, name="rounded%d_%d" % (n, half), tag="rounded", bufs=6, align_bytes=64)
             if engines == ("vector", "vector"):
                 evac(
                     engines[0],
@@ -288,51 +288,80 @@ def tile_featurepairqkscoreattribution_x2_kernel(
                         results[n, half][:, s, :].rearrange("f (p u e) -> f u p e", u=2, e=2),
                     )
 
-        def turn_result(n, half, engine="scalar"):
+        def turn_result_tile(n, half, s, engine):
             words = rounded[n, half][:].bitcast(F32)
             bank = next_bank()
-            for su in range(4):
-                nc.tensor.transpose(bank[:, P * su : P * (su + 1)], words[:, P * su : P * (su + 1)], ident[:])
-            plane_in[n, half] = flow.tile([P, 4 * PAIR], BF16, name="plane_in%d_%d" % (n, half), tag="plane_in", bufs=7, align_bytes=64)
+            for u in range(2):
+                nc.tensor.transpose(bank[:, P * u : P * (u + 1)], words[:, P * (2 * s + u) : P * (2 * s + u + 1)], ident[:])
+            if s == 0:
+                plane_in[n, half] = flow.tile([P, 4 * PAIR], BF16, name="plane_in%d_%d" % (n, half), tag="plane_in", bufs=8, align_bytes=64)
             evac(
                 engine,
-                plane_in[n, half][:].bitcast(F32).rearrange("p (s f u) -> p s f u", s=2, u=2),
-                bank[:].rearrange("p (s u f) -> p s f u", s=2, u=2),
+                plane_in[n, half][:, HALF * s : HALF * (s + 1)].bitcast(F32).rearrange("p (f u) -> p f u", u=2),
+                bank[:, 0:PAIR].rearrange("p (u f) -> p f u", u=2),
             )
 
-        def quantize_result(n, half):
-            cols = slice(PAIR * n, PAIR * (n + 1))
+        def quantize_result_tile(n, half, s):
+            cols = slice(PAIR * n + P * s, PAIR * n + P * (s + 1))
             nc.vector.quantize_mx(
                 out=plane_codes[:, half, cols].bitcast(FP8X4),
                 scales=plane_scales[4 * half : P, cols],
-                in_=plane_in[n, half][:],
+                in_=plane_in[n, half][:, HALF * s : HALF * (s + 1)],
             )
             nc.sync.dma_start(
                 out=out_1[half, :, cols, :].rearrange("p f t -> p (f t)").bitcast(I32),
                 in_=plane_codes[:, half, cols].bitcast(I32),
             )
 
-        def store_scales():
+        def turn_result(n, half, engine="scalar"):
+            words = rounded[n, half][:].bitcast(F32)
+            bank = next_bank()
+            for su in range(4):
+                nc.tensor.transpose(bank[:, P * su : P * (su + 1)], words[:, P * su : P * (su + 1)], ident[:])
+            plane_in[n, half] = flow.tile([P, 4 * PAIR], BF16, name="plane_in%d_%d" % (n, half), tag="plane_in", bufs=8, align_bytes=64)
+            evac(
+                engine,
+                plane_in[n, half][:].bitcast(F32).rearrange("p (s f u) -> p s f u", s=2, u=2),
+                bank[:].rearrange("p (s u f) -> p s f u", s=2, u=2),
+            )
+
+        def quantize_result(n, half, first=None):
+            cols = slice(PAIR * n, PAIR * (n + 1))
+            nc.vector.quantize_mx(
+                out=plane_codes[:, half, cols].bitcast(FP8X4),
+                scales=plane_scales[4 * half : P, cols],
+                in_=plane_in[n, half][:],
+            )
+            if first == "later":
+                return
+            if first is not None:
+                cols = slice(PAIR * first, PAIR * (n + 1))
+            nc.sync.dma_start(
+                out=out_1[half, :, cols, :].rearrange("p f t -> p (f t)").bitcast(I32),
+                in_=plane_codes[:, half, cols].bitcast(I32),
+            )
+
+        def store_scales(queue, cols):
             for quad in range(4):
-                nc.scalar.dma_start(
-                    out=out_2[:, 4 * quad : 4 * quad + 4, :].bitcast(I32),
-                    in_=plane_scales[32 * quad : 32 * quad + 8, :].bitcast(I32),
+                queue.dma_start(
+                    out=out_2[:, 4 * quad : 4 * quad + 4, cols].bitcast(I32),
+                    in_=plane_scales[32 * quad : 32 * quad + 8, cols].bitcast(I32),
                 )
 
         SV = ("scalar", "vector")
         VS = ("vector", "scalar")
         SS = ("scalar", "scalar")
         VV = ("vector", "vector")
-        warm(5)
-        turn("k", 0, SV)
-        warm(4)
-        quantize_turned("k", 0, True)
+        warm(8)
         sort_weight("k")
+        turn("k", 0, SV)
+        warm(6)
+        quantize_turned("k", 0, True)
         turn("k", 1)
         project("k", 0)
         weigh_tokens(0)
-        quantize_turned("k", 1)
         group_tokens("k", 0)
+        quantize_turned("k", 1)
         turn("q", 0)
         project("k", 1)
         sort_weight("q")
@@ -340,74 +369,75 @@ def tile_featurepairqkscoreattribution_x2_kernel(
         quantize_turned("q", 0)
         group_tokens("q", 0)
         quantize_projected("k", 0)
-        turn("q", 1)
+        turn("k", 2)
         project("q", 0)
         quantize_tokens("q", 0)
         quantize_projected("k", 1)
-        quantize_turned("q", 1)
+        quantize_turned("k", 2)
         coactivate(0, 0)
         weigh_tokens(1)
         quantize_projected("q", 0)
         group_tokens("k", 1)
-        turn("k", 2)
-        score(0, 0)
-        project("q", 1)
-        coactivate(1, 0)
-        quantize_turned("k", 2)
-        quantize_tokens("k", 1)
-        quantize_projected("q", 1)
-        group_tokens("q", 1)
         turn("k", 3)
-        score(1, 0)
+        score(0, 0)
         project("k", 2)
-        coactivate(0, 1)
-        coactivate(1, 1)
+        coactivate(1, 0)
         quantize_turned("k", 3)
-        round_result(0, 0)
-        quantize_tokens("q", 1)
-        round_result(1, 0)
-        turn("q", 2, VV)
-        turn("q", 3, SV)
-        turn_result(0, 0)
-        turn_result(1, 0)
-        quantize_projected("k", 2)
-        quantize_turned("q", 2)
+        quantize_tokens("k", 1)
+        group_tokens("q", 1)
+        turn("q", 1, SV)
         project("k", 3)
-        quantize_turned("q", 3)
-        quantize_result(0, 0)
-        project("q", 2)
+        coactivate(0, 1)
+        quantize_projected("k", 2)
+        quantize_turned("q", 1)
+        round_result(0, 0)
         quantize_projected("k", 3)
-        quantize_result(1, 0)
-        coactivate(2, 0, VS)
+        quantize_tokens("q", 1)
+        turn("q", 2, SV)
+        turn_result(0, 0)
         score(0, 1)
-        coactivate(2, 1)
-        quantize_projected("q", 2)
+        project("q", 1)
+        coactivate(1, 1)
+        quantize_turned("q", 2)
+        round_result(0, 1)
+        quantize_projected("q", 1)
+        quantize_result(0, 0)
+        turn("q", 3)
+        turn_result(0, 1, "vector")
+        score(1, 0)
+        coactivate(2, 0)
+        quantize_turned("q", 3)
         score(1, 1)
-        round_result(0, 1, SV)
+        project("q", 2)
+        round_result(1, 0)
+        quantize_result(0, 1)
         project("q", 3)
-        score(2, 0)
-        coactivate(3, 0)
+        quantize_projected("q", 2)
         round_result(1, 1)
+        coactivate(2, 1)
         quantize_projected("q", 3)
+        score(2, 0)
+        round_result(2, 0, ("gpsimd", "gpsimd"))
+        coactivate(3, 0)
         score(2, 1)
+        round_result(2, 1, ("gpsimd", "gpsimd"))
         coactivate(3, 1)
-        round_result(2, 0, SS)
-        turn_result(0, 1)
-        turn_result(1, 1)
-        round_result(2, 1, SV)
         score(3, 0)
         score(3, 1)
         round_result(3, 0, SV)
+
+        turn_result(1, 0)
+        turn_result(1, 1)
         turn_result(2, 0)
-        warm(5)
+        warm(6)
         turn_result(2, 1)
-        round_result(3, 1, ("vector", "vector", "split"))
-        quantize_result(0, 1)
+        round_result(3, 1)
         turn_result(3, 0)
-        quantize_result(1, 1)
+        quantize_result(1, 0)
         turn_result(3, 1)
         quantize_result(2, 0)
-        quantize_result(3, 0)
+        quantize_result(1, 1)
         quantize_result(2, 1)
+        quantize_result(3, 0)
         quantize_result(3, 1)
-        store_scales()
+        store_scales(nc.scalar, slice(0, F))

@@ -20,8 +20,13 @@ MULT = mybir.AluOpType.mult
 P = 128
 HALF = 512
 PAIR = 256
+QUADRANT = 32
 BANKS = 8
 OUT_FACTOR = 1.0 / (math.sqrt(A // H) * T)
+
+SCALAR = ("scalar", "scalar")
+SHARED = ("scalar", "vector")
+GPSIMD = ("gpsimd", "gpsimd")
 
 
 def tile_featurepairqkscoreattribution_x2_kernel(
@@ -37,9 +42,9 @@ def tile_featurepairqkscoreattribution_x2_kernel(
         banks_taken = []
 
         def next_bank():
-            n = len(banks_taken)
-            banks_taken.append(n)
-            return psum.tile([P, HALF], F32, name="bank%d" % n, tag="bank%d" % (n % BANKS))
+            count = len(banks_taken)
+            banks_taken.append(count)
+            return psum.tile([P, HALF], F32, name="bank%d" % count, tag="bank%d" % (count % BANKS))
 
         def operand(name, width):
             codes = keep.tile([P, width], U32, name=name + "_codes", align_bytes=256)
@@ -50,24 +55,38 @@ def tile_featurepairqkscoreattribution_x2_kernel(
             codes, scales = target
             nc.vector.quantize_mx(out=codes[:, cols].bitcast(FP8X4), scales=scales[:, cols], in_=values)
 
+        def move(engine, out, in_):
+            if engine == "vector":
+                nc.vector.tensor_copy(out=out, in_=in_)
+            elif engine == "gpsimd":
+                nc.gpsimd.tensor_scalar(out=out, in0=in_, scalar1=1.0, scalar2=1.0, op0=MULT, op1=MULT)
+            else:
+                nc.scalar.copy(out=out, in_=in_)
+
+        def product(target, stationary, first, moving):
+            cols = slice(first, first + P)
+            nc.tensor.matmul_mx(
+                out=target,
+                lhsT=stationary[0][:, cols].bitcast(FP8X4),
+                lhsT_scale=stationary[1][:, cols],
+                rhs=moving[0][:].bitcast(FP8X4),
+                rhs_scale=moving[1][:],
+                start=True,
+                stop=True,
+            )
 
         head_row = keep.tile([P, H], BF16, name="head_row")
         nc.scalar.dma_start(out=head_row[:], in_=head_w.partition_broadcast(P))
         g_rows = keep.tile([P, 4], BF16, name="g_rows")
         head_col = keep.tile([P, 1], F32, name="head_col")
-        for h in range(H):
-            rows = slice(32 * h, 32 * h + 32)
-            nc.scalar.activation(out=head_col[rows, :], in_=head_row[rows, h : h + 1], func=COPY)
+        for head in range(H):
+            rows = slice(QUADRANT * head, QUADRANT * (head + 1))
+            nc.scalar.activation(out=head_col[rows, :], in_=head_row[rows, head : head + 1], func=COPY)
 
-        warm_in = keep.tile([P, 4 * PAIR], BF16, name="warm_in", align_bytes=64)
-        nc.gpsimd.memset(warm_in[:].bitcast(I32), 0)
-        raw_scales = {}
-        for side in ("k", "q"):
-            raw_scales[side] = keep.tile([P, 2, A], U8, name="raw_scales_" + side, align_bytes=64)
-            nc.vector.memset(raw_scales[side][:].bitcast(I32), 0)
-            if side == "k":
-                warm_mx = operand("warm", PAIR)
-                quantize(warm_mx, slice(0, PAIR), warm_in[:])
+        raw_scales = {"k": keep.tile([P, 2, A], U8, name="raw_scales_k", align_bytes=64)}
+        nc.vector.memset(raw_scales["k"][:].bitcast(I32), 0)
+        raw_scales["q"] = keep.tile([P, 2, A], U8, name="raw_scales_q", align_bytes=64)
+        nc.vector.memset(raw_scales["q"][:].bitcast(I32), 0)
 
         ident = keep.tile([P, P], F32, name="ident")
         make_identity(nc, ident[:])
@@ -77,67 +96,54 @@ def tile_featurepairqkscoreattribution_x2_kernel(
         tokens = {}
 
         def load_directions(side, n):
-            src = dq if side == "q" else dk
-            pair = keep.tile([P, 2, D], BF16, name="dir_%s%d" % (side, n), align_bytes=64)
-            nc.sync.dma_start(out=pair[:], in_=src[PAIR * n : PAIR * (n + 1), :].rearrange("(s p) d -> p s d", p=P))
+            source = dq if side == "q" else dk
+            both = keep.tile([P, 2, D], BF16, name="dir_%s%d" % (side, n), align_bytes=64)
+            nc.sync.dma_start(out=both[:], in_=source[PAIR * n : PAIR * (n + 1), :].rearrange("(s p) d -> p s d", p=P))
             for s in range(2):
-                directions[side, n, s] = pair[:, s, :]
+                directions[side, n, s] = both[:, s, :]
 
-        def load_directions_singly(side, n):
-            src = dq if side == "q" else dk
-            for s in range(2):
-                single = keep.tile([P, D], BF16, name="dir_%s%d_%d" % (side, n, s), align_bytes=64)
-                nc.sync.dma_start(out=single[:], in_=src[PAIR * n + P * s : PAIR * n + P * (s + 1), :])
-                directions[side, n, s] = single[:]
-
-        def load_words(side):
-            src = wq_words if side == "q" else wk_words
+        def load_weight_words(side):
+            source = wq_words if side == "q" else wk_words
             raw_words[side] = keep.tile([P, 2, 2 * A], U8, name="raw_words_" + side, align_bytes=64)
-            nc.sync.dma_start(out=raw_words[side][:].bitcast(I32), in_=src.rearrange("g p n -> p g n").bitcast(I32))
+            nc.sync.dma_start(out=raw_words[side][:].bitcast(I32), in_=source.rearrange("g p n -> p g n").bitcast(I32))
 
-        def load_scales(side, quadrants):
-            src = wq_scales if side == "q" else wk_scales
-            for quad in quadrants:
+        def load_weight_scales(side):
+            source = wq_scales if side == "q" else wk_scales
+            for quad in range(4):
                 nc.sync.dma_start(
-                    out=raw_scales[side][32 * quad : 32 * quad + 4, :, :].bitcast(I32),
-                    in_=src[:, 4 * quad : 4 * quad + 4, :].rearrange("g r n -> r g n").bitcast(I32),
+                    out=raw_scales[side][QUADRANT * quad : QUADRANT * quad + 4, :, :].bitcast(I32),
+                    in_=source[:, 4 * quad : 4 * quad + 4, :].rearrange("g r n -> r g n").bitcast(I32),
                 )
 
         def load_tokens(side, half):
-            src = aq if side == "q" else ak
+            source = aq if side == "q" else ak
             tokens[side, half] = keep.tile([P, 4, HALF], BF16, name="tok_%s%d" % (side, half), align_bytes=64)
-            nc.sync.dma_start(out=tokens[side, half][:], in_=src[:, HALF * half : HALF * (half + 1)].rearrange("(p t) n -> p t n", t=4))
+            nc.sync.dma_start(
+                out=tokens[side, half][:],
+                in_=source[:, HALF * half : HALF * (half + 1)].rearrange("(p t) n -> p t n", t=4),
+            )
 
-        load_directions_singly("k", 0)
-        load_scales("k", range(4))
-        load_words("k")
+        for s in range(2):
+            single = keep.tile([P, D], BF16, name="dir_k0_%d" % s, align_bytes=64)
+            nc.sync.dma_start(out=single[:], in_=dk[P * s : P * (s + 1), :])
+            directions["k", 0, s] = single[:]
+        load_weight_scales("k")
+        load_weight_words("k")
         load_directions("k", 1)
         nc.sync.dma_start(out=g_rows[:], in_=g.rearrange("(p t) -> p t", t=4))
         load_tokens("k", 0)
         load_directions("q", 0)
-        load_words("q")
-        load_scales("q", range(4))
+        load_weight_words("q")
+        load_weight_scales("q")
         load_tokens("q", 0)
         load_directions("k", 2)
         load_tokens("k", 1)
         load_directions("k", 3)
         load_tokens("q", 1)
-        load_directions("q", 1)
-        load_directions("q", 2)
-        load_directions("q", 3)
+        for n in range(1, 4):
+            load_directions("q", n)
 
         weights = {}
-
-        def sort_weight(side):
-            words = keep.tile([P, 2, 2 * A], U8, name="words_" + side, align_bytes=256)
-            scales = keep.tile([P, 2, A], U8, name="scales_" + side, align_bytes=256)
-            for target, source in ((words, raw_words[side]), (scales, raw_scales[side])):
-                nc.vector.tensor_copy(
-                    out=target[:].bitcast(I32).rearrange("p g (t b w) -> p g t b w", t=4, b=16),
-                    in_=source[:].bitcast(I32).rearrange("p g (b t w) -> p g t b w", t=4, b=16),
-                )
-            weights[side] = (words, scales)
-
         turned = {}
         dir_mx = {}
         projected = {}
@@ -153,45 +159,43 @@ def tile_featurepairqkscoreattribution_x2_kernel(
         plane_codes = keep.tile([P, 2, F], U32, name="plane_codes", align_bytes=256)
         plane_scales = keep.tile([P, F], U8, name="plane_scales", align_bytes=256)
 
-        def warm(count):
-            bank = next_bank()
-            for rep in range(count):
-                product(bank[:, 0:PAIR], warm_mx, 0, warm_mx)
+        def sort_weight(side):
+            words = keep.tile([P, 2, 2 * A], U8, name="words_" + side, align_bytes=256)
+            scales = keep.tile([P, 2, A], U8, name="scales_" + side, align_bytes=256)
+            for target, source in ((words, raw_words[side]), (scales, raw_scales[side])):
+                nc.vector.tensor_copy(
+                    out=target[:].bitcast(I32).rearrange("p g (t b w) -> p g t b w", t=4, b=16),
+                    in_=source[:].bitcast(I32).rearrange("p g (b t w) -> p g t b w", t=4, b=16),
+                )
+            weights[side] = (words, scales)
 
-        def evac(engine, out, in_):
-            if engine == "vector":
-                nc.vector.tensor_copy(out=out, in_=in_)
-            elif engine == "gpsimd":
-                nc.gpsimd.tensor_scalar(out=out, in0=in_, scalar1=1.0, scalar2=1.0, op0=MULT, op1=MULT)
-            else:
-                nc.scalar.copy(out=out, in_=in_)
-
-        def turn(side, n, engines=("scalar", "scalar")):
+        def turn(side, n, engines=SCALAR):
             turned[side, n] = flow.tile([P, 2 * D], BF16, name="turned_%s%d" % (side, n), tag="turned", align_bytes=64)
             for s in range(2):
-                words = directions[side, n, s].bitcast(F32)
+                doubles = directions[side, n, s].bitcast(F32)
                 bank = next_bank()
-                for gu in range(4):
-                    first = 256 * (gu // 2) + gu % 2
-                    nc.tensor.transpose(bank[:, P * gu : P * (gu + 1)], words[:, first : 256 * (gu // 2 + 1) : 2], ident[:])
-                evac(
+                for grp in range(2):
+                    for u in range(2):
+                        place = P * (2 * grp + u)
+                        every_second = doubles[:, PAIR * grp + u : PAIR * (grp + 1) : 2]
+                        nc.tensor.transpose(bank[:, place : place + P], every_second, ident[:])
+                move(
                     engines[s],
                     turned[side, n][:, D * s : D * (s + 1)].bitcast(F32).rearrange("p (g f u) -> p g f u", g=2, u=2),
                     bank[:].rearrange("p (g u f) -> p g f u", g=2, u=2),
                 )
 
-        def quantize_turned(side, n, split=False):
+        def quantize_turned(side, n, pieces=1):
             codes = flow.tile([P, HALF], U32, name="dir_codes_%s%d" % (side, n), tag="dir_codes", align_bytes=256)
             scales = flow.tile([P, HALF], U8, name="dir_scales_%s%d" % (side, n), tag="dir_scales", align_bytes=256)
             dir_mx[side, n] = (codes, scales)
-            if split:
-                for s in range(2):
-                    quantize(dir_mx[side, n], slice(PAIR * s, PAIR * (s + 1)), turned[side, n][:, D * s : D * (s + 1)])
-            else:
-                quantize(dir_mx[side, n], slice(0, HALF), turned[side, n][:])
+            width = HALF // pieces
+            for piece in range(pieces):
+                cols = slice(width * piece, width * (piece + 1))
+                quantize(dir_mx[side, n], cols, turned[side, n][:, 4 * cols.start : 4 * cols.stop])
 
         def project(side, n):
-            words, wscales = weights[side]
+            words, word_scales = weights[side]
             codes, scales = dir_mx[side, n]
             projected[side, n] = flow.tile([P, 4 * PAIR], BF16, name="proj_%s%d" % (side, n), tag="proj", align_bytes=64)
             for s in range(2):
@@ -202,7 +206,7 @@ def tile_featurepairqkscoreattribution_x2_kernel(
                         nc.tensor.matmul_mx(
                             out=bank[:, P * t : P * (t + 1)],
                             lhsT=words[:, grp, 2 * P * t : 2 * P * (t + 1)].bitcast(FP4X4),
-                            lhsT_scale=wscales[:, grp, P * t : P * (t + 1)],
+                            lhsT_scale=word_scales[:, grp, P * t : P * (t + 1)],
                             rhs=codes[:, cols].bitcast(FP8X4),
                             rhs_scale=scales[:, cols],
                             start=(grp == 0),
@@ -215,11 +219,8 @@ def tile_featurepairqkscoreattribution_x2_kernel(
                 else:
                     nc.scalar.copy(out=target, in_=source)
 
-        def quantize_projected(side, n, split=False):
-            if split:
-                for s in range(2):
-                    quantize(proj_mx["q", n], slice(P * s, P * (s + 1)), projected[side, n][:, HALF * s : HALF * (s + 1)])
-            elif side == "q":
+        def quantize_projected(side, n):
+            if side == "q":
                 quantize(proj_mx["q", n], slice(0, PAIR), projected[side, n][:])
             else:
                 quantize(proj_mx["k", n // 2], slice(PAIR * (n % 2), PAIR * (n % 2 + 1)), projected[side, n][:])
@@ -227,11 +228,15 @@ def tile_featurepairqkscoreattribution_x2_kernel(
         def weigh_tokens(half):
             weighed = flow.tile([P, 4, HALF], BF16, name="weighed%d" % half, tag="weighed", align_bytes=64)
             for t in range(4):
-                nc.vector.tensor_scalar(out=weighed[:, t, :], in0=tokens["k", half][:, t, :], scalar1=g_rows[:, t : t + 1], scalar2=None, op0=MULT)
+                nc.vector.tensor_scalar(
+                    out=weighed[:, t, :], in0=tokens["k", half][:, t, :], scalar1=g_rows[:, t : t + 1], scalar2=None, op0=MULT
+                )
             tokens["k", half] = weighed
 
         def group_tokens(side, half):
-            tok_grouped[side, half] = flow.tile([P, 4 * HALF], BF16, name="grouped_%s%d" % (side, half), tag="grouped", align_bytes=64)
+            tok_grouped[side, half] = flow.tile(
+                [P, 4 * HALF], BF16, name="grouped_%s%d" % (side, half), tag="grouped", align_bytes=64
+            )
             nc.vector.tensor_copy(
                 out=tok_grouped[side, half][:].rearrange("p (c i t) -> p c t i", i=4, t=4),
                 in_=tokens[side, half][:].rearrange("p t (c i) -> p c t i", i=4),
@@ -240,128 +245,87 @@ def tile_featurepairqkscoreattribution_x2_kernel(
         def quantize_tokens(side, half):
             quantize(tok_mx[side, half], slice(0, HALF), tok_grouped[side, half][:])
 
-        def product(bank, stationary, first, moving):
-            cols = slice(first, first + P)
-            nc.tensor.matmul_mx(
-                out=bank[:],
-                lhsT=stationary[0][:, cols].bitcast(FP8X4),
-                lhsT_scale=stationary[1][:, cols],
-                rhs=moving[0][:].bitcast(FP8X4),
-                rhs_scale=moving[1][:],
-                start=True,
-                stop=True,
-            )
-
-        def coactivate(n, half, engines=("scalar", "scalar")):
+        def coactivate(n, half):
             coact[n, half] = flow.tile([P, 2, HALF], F32, name="coact%d_%d" % (n, half), tag="coact", bufs=5)
             for s in range(2):
                 bank = next_bank()
-                product(bank, tok_mx["q", n // 2], PAIR * (n % 2) + P * s, tok_mx["k", half])
-                evac(engines[s], coact[n, half][:, s, :], bank[:])
+                product(bank[:], tok_mx["q", n // 2], PAIR * (n % 2) + P * s, tok_mx["k", half])
+                nc.scalar.copy(out=coact[n, half][:, s, :], in_=bank[:])
 
         def score(n, half):
             results[n, half] = flow.tile([P, 2, HALF], F32, name="result%d_%d" % (n, half), tag="result", bufs=4)
             for s in range(2):
                 bank = next_bank()
-                product(bank, proj_mx["q", n], P * s, proj_mx["k", half])
+                product(bank[:], proj_mx["q", n], P * s, proj_mx["k", half])
                 nc.vector.scalar_tensor_tensor(
-                    out=results[n, half][:, s, :], in0=bank[:], scalar=OUT_FACTOR, in1=coact[n, half][:, s, :], op0=MULT, op1=MULT
+                    out=results[n, half][:, s, :],
+                    in0=bank[:],
+                    scalar=OUT_FACTOR,
+                    in1=coact[n, half][:, s, :],
+                    op0=MULT,
+                    op1=MULT,
                 )
             nc.sync.dma_start(
                 out=out_0[PAIR * n : PAIR * (n + 1), HALF * half : HALF * (half + 1)].rearrange("(s p) j -> p s j", p=P),
                 in_=results[n, half][:],
             )
 
-        def round_result(n, half, engines=("vector", "vector")):
-            rounded[n, half] = flow.tile([P, 2 * HALF], BF16, name="rounded%d_%d" % (n, half), tag="rounded", bufs=6, align_bytes=64)
-            if engines == ("vector", "vector"):
-                evac(
-                    engines[0],
-                    rounded[n, half][:].rearrange("f (s u p e) -> f s u p e", s=2, u=2, e=2),
-                    results[n, half][:].rearrange("f s (p u e) -> f s u p e", u=2, e=2),
+        def rounded_tile(n, half):
+            rounded[n, half] = flow.tile(
+                [P, 2 * HALF], BF16, name="rounded%d_%d" % (n, half), tag="rounded", bufs=6, align_bytes=64
+            )
+            return rounded[n, half]
+
+        def round_result(n, half):
+            nc.vector.tensor_copy(
+                out=rounded_tile(n, half)[:].rearrange("f (s u p e) -> f s u p e", s=2, u=2, e=2),
+                in_=results[n, half][:].rearrange("f s (p u e) -> f s u p e", u=2, e=2),
+            )
+
+        def round_result_by_tile(n, half, engines):
+            target = rounded_tile(n, half)
+            for s in range(2):
+                move(
+                    engines[s],
+                    target[:, HALF * s : HALF * (s + 1)].rearrange("f (u p e) -> f u p e", u=2, e=2),
+                    results[n, half][:, s, :].rearrange("f (p u e) -> f u p e", u=2, e=2),
                 )
-            else:
-                for s in range(2):
-                    evac(
-                        engines[s],
-                        rounded[n, half][:, HALF * s : HALF * (s + 1)].rearrange("f (u p e) -> f u p e", u=2, e=2),
-                        results[n, half][:, s, :].rearrange("f (p u e) -> f u p e", u=2, e=2),
-                    )
 
-        def turn_result_tile(n, half, s, engine):
-            words = rounded[n, half][:].bitcast(F32)
+        def turn_result(n, half):
+            doubles = rounded[n, half][:].bitcast(F32)
             bank = next_bank()
-            for u in range(2):
-                nc.tensor.transpose(bank[:, P * u : P * (u + 1)], words[:, P * (2 * s + u) : P * (2 * s + u + 1)], ident[:])
-            if s == 0:
-                plane_in[n, half] = flow.tile([P, 4 * PAIR], BF16, name="plane_in%d_%d" % (n, half), tag="plane_in", bufs=8, align_bytes=64)
-            evac(
-                engine,
-                plane_in[n, half][:, HALF * s : HALF * (s + 1)].bitcast(F32).rearrange("p (f u) -> p f u", u=2),
-                bank[:, 0:PAIR].rearrange("p (u f) -> p f u", u=2),
+            for place in range(0, HALF, P):
+                nc.tensor.transpose(bank[:, place : place + P], doubles[:, place : place + P], ident[:])
+            plane_in[n, half] = flow.tile(
+                [P, 4 * PAIR], BF16, name="plane_in%d_%d" % (n, half), tag="plane_in", bufs=8, align_bytes=64
+            )
+            nc.scalar.copy(
+                out=plane_in[n, half][:].bitcast(F32).rearrange("p (s f u) -> p s f u", s=2, u=2),
+                in_=bank[:].rearrange("p (s u f) -> p s f u", s=2, u=2),
             )
 
-        def quantize_result_tile(n, half, s):
-            cols = slice(PAIR * n + P * s, PAIR * n + P * (s + 1))
-            nc.vector.quantize_mx(
-                out=plane_codes[:, half, cols].bitcast(FP8X4),
-                scales=plane_scales[4 * half : P, cols],
-                in_=plane_in[n, half][:, HALF * s : HALF * (s + 1)],
-            )
-            nc.sync.dma_start(
-                out=out_1[half, :, cols, :].rearrange("p f t -> p (f t)").bitcast(I32),
-                in_=plane_codes[:, half, cols].bitcast(I32),
-            )
-
-        def turn_result(n, half, engine="scalar"):
-            words = rounded[n, half][:].bitcast(F32)
-            bank = next_bank()
-            for su in range(4):
-                nc.tensor.transpose(bank[:, P * su : P * (su + 1)], words[:, P * su : P * (su + 1)], ident[:])
-            plane_in[n, half] = flow.tile([P, 4 * PAIR], BF16, name="plane_in%d_%d" % (n, half), tag="plane_in", bufs=8, align_bytes=64)
-            evac(
-                engine,
-                plane_in[n, half][:].bitcast(F32).rearrange("p (s f u) -> p s f u", s=2, u=2),
-                bank[:].rearrange("p (s u f) -> p s f u", s=2, u=2),
-            )
-
-        def quantize_result(n, half, first=None):
+        def quantize_result(n, half):
             cols = slice(PAIR * n, PAIR * (n + 1))
             nc.vector.quantize_mx(
                 out=plane_codes[:, half, cols].bitcast(FP8X4),
                 scales=plane_scales[4 * half : P, cols],
                 in_=plane_in[n, half][:],
             )
-            if first == "later":
-                return
-            if first is not None:
-                cols = slice(PAIR * first, PAIR * (n + 1))
             nc.sync.dma_start(
                 out=out_1[half, :, cols, :].rearrange("p f t -> p (f t)").bitcast(I32),
                 in_=plane_codes[:, half, cols].bitcast(I32),
             )
 
-        def store_scales(queue, cols):
-            for quad in range(4):
-                queue.dma_start(
-                    out=out_2[:, 4 * quad : 4 * quad + 4, cols].bitcast(I32),
-                    in_=plane_scales[32 * quad : 32 * quad + 8, cols].bitcast(I32),
-                )
-
-        SV = ("scalar", "vector")
-        VS = ("vector", "scalar")
-        SS = ("scalar", "scalar")
-        VV = ("vector", "vector")
-        warm(8)
         sort_weight("k")
-        turn("k", 0, SV)
-        warm(6)
-        quantize_turned("k", 0, True)
+        turn("k", 0, SHARED)
+        quantize_turned("k", 0, pieces=2)
+
         turn("k", 1)
         project("k", 0)
         weigh_tokens(0)
         group_tokens("k", 0)
         quantize_turned("k", 1)
+
         turn("q", 0)
         project("k", 1)
         sort_weight("q")
@@ -369,6 +333,7 @@ def tile_featurepairqkscoreattribution_x2_kernel(
         quantize_turned("q", 0)
         group_tokens("q", 0)
         quantize_projected("k", 0)
+
         turn("k", 2)
         project("q", 0)
         quantize_tokens("q", 0)
@@ -378,6 +343,7 @@ def tile_featurepairqkscoreattribution_x2_kernel(
         weigh_tokens(1)
         quantize_projected("q", 0)
         group_tokens("k", 1)
+
         turn("k", 3)
         score(0, 0)
         project("k", 2)
@@ -385,15 +351,17 @@ def tile_featurepairqkscoreattribution_x2_kernel(
         quantize_turned("k", 3)
         quantize_tokens("k", 1)
         group_tokens("q", 1)
-        turn("q", 1, SV)
+
+        turn("q", 1)
         project("k", 3)
         coactivate(0, 1)
         quantize_projected("k", 2)
-        quantize_turned("q", 1)
         round_result(0, 0)
+        quantize_turned("q", 1)
         quantize_projected("k", 3)
         quantize_tokens("q", 1)
-        turn("q", 2, SV)
+
+        turn("q", 2, SHARED)
         turn_result(0, 0)
         score(0, 1)
         project("q", 1)
@@ -402,8 +370,9 @@ def tile_featurepairqkscoreattribution_x2_kernel(
         round_result(0, 1)
         quantize_projected("q", 1)
         quantize_result(0, 0)
-        turn("q", 3)
-        turn_result(0, 1, "vector")
+
+        turn("q", 3, SHARED)
+        turn_result(0, 1)
         score(1, 0)
         coactivate(2, 0)
         quantize_turned("q", 3)
@@ -416,28 +385,28 @@ def tile_featurepairqkscoreattribution_x2_kernel(
         round_result(1, 1)
         coactivate(2, 1)
         quantize_projected("q", 3)
-        score(2, 0)
-        round_result(2, 0, ("gpsimd", "gpsimd"))
-        coactivate(3, 0)
-        score(2, 1)
-        round_result(2, 1, ("gpsimd", "gpsimd"))
-        coactivate(3, 1)
+
+        for half in range(2):
+            score(2, half)
+            round_result_by_tile(2, half, GPSIMD)
+            coactivate(3, half)
         score(3, 0)
         score(3, 1)
-        round_result(3, 0, SV)
+        round_result_by_tile(3, 0, SHARED)
 
         turn_result(1, 0)
         turn_result(1, 1)
         turn_result(2, 0)
-        warm(6)
         turn_result(2, 1)
         round_result(3, 1)
         turn_result(3, 0)
         quantize_result(1, 0)
         turn_result(3, 1)
-        quantize_result(2, 0)
-        quantize_result(1, 1)
-        quantize_result(2, 1)
-        quantize_result(3, 0)
-        quantize_result(3, 1)
-        store_scales(nc.scalar, slice(0, F))
+        for n, half in ((2, 0), (1, 1), (3, 0), (2, 1), (3, 1)):
+            quantize_result(n, half)
+
+        for quad in range(4):
+            nc.scalar.dma_start(
+                out=out_2[:, 4 * quad : 4 * quad + 4, :].bitcast(I32),
+                in_=plane_scales[QUADRANT * quad : QUADRANT * quad + 8, :].bitcast(I32),
+            )

import math
from contextlib import ExitStack

import concourse.mybir as mybir
from concourse.masks import make_identity

F, J, D, A, H, T = 1024, 1024, 1024, 512, 4, 512
FLOPS = 2 * F * D * A + 2 * J * D * A + 2 * F * J * A + 2 * F * J * T

F32 = mybir.dt.float32
BF16 = mybir.dt.bfloat16
I32 = mybir.dt.int32
U32 = mybir.dt.uint32
U8 = mybir.dt.uint8
FP8X4 = mybir.dt.float8_e4m3fn_x4
FP4X4 = mybir.dt.float4_e2m1fn_x4
COPY = mybir.ActivationFunctionType.Copy
MULT = mybir.AluOpType.mult

P = 128
HALF = 512
PAIR = 256
QUADRANT = 32
BANKS = 8
OUT_FACTOR = 1.0 / (math.sqrt(A // H) * T)

SCALAR = ("scalar", "scalar")
SHARED = ("scalar", "vector")
GPSIMD = ("gpsimd", "gpsimd")


def tile_featurepairqkscoreattribution_x2_kernel(
    tc, dq, dk, wq_words, wq_scales, wk_words, wk_scales, head_w, aq, ak, g, out_0, out_1, out_2
):
    nc = tc.nc
    with ExitStack() as ctx:
        keep = ctx.enter_context(tc.tile_pool(name="keep", bufs=1))
        flow = ctx.enter_context(tc.tile_pool(name="flow", bufs=3))
        psum = ctx.enter_context(tc.psum_pool(name="psum", bufs=1))
        ctx.enter_context(tc.manual_schedule())

        banks_taken = []

        def next_bank():
            count = len(banks_taken)
            banks_taken.append(count)
            return psum.tile([P, HALF], F32, name="bank%d" % count, tag="bank%d" % (count % BANKS))

        def operand(name, width):
            codes = keep.tile([P, width], U32, name=name + "_codes", align_bytes=256)
            scales = keep.tile([P, width], U8, name=name + "_scales", align_bytes=256)
            return codes, scales

        def quantize(target, cols, values):
            codes, scales = target
            nc.vector.quantize_mx(out=codes[:, cols].bitcast(FP8X4), scales=scales[:, cols], in_=values)

        def move(engine, out, in_):
            if engine == "vector":
                nc.vector.tensor_copy(out=out, in_=in_)
            elif engine == "gpsimd":
                nc.gpsimd.tensor_scalar(out=out, in0=in_, scalar1=1.0, scalar2=1.0, op0=MULT, op1=MULT)
            else:
                nc.scalar.copy(out=out, in_=in_)

        def product(target, stationary, first, moving):
            cols = slice(first, first + P)
            nc.tensor.matmul_mx(
                out=target,
                lhsT=stationary[0][:, cols].bitcast(FP8X4),
                lhsT_scale=stationary[1][:, cols],
                rhs=moving[0][:].bitcast(FP8X4),
                rhs_scale=moving[1][:],
                start=True,
                stop=True,
            )

        head_row = keep.tile([P, H], BF16, name="head_row")
        nc.scalar.dma_start(out=head_row[:], in_=head_w.partition_broadcast(P))
        g_rows = keep.tile([P, 4], BF16, name="g_rows")
        head_col = keep.tile([P, 1], F32, name="head_col")
        for head in range(H):
            rows = slice(QUADRANT * head, QUADRANT * (head + 1))
            nc.scalar.activation(out=head_col[rows, :], in_=head_row[rows, head : head + 1], func=COPY)

        raw_scales = {"k": keep.tile([P, 2, A], U8, name="raw_scales_k", align_bytes=64)}
        nc.vector.memset(raw_scales["k"][:].bitcast(I32), 0)
        raw_scales["q"] = keep.tile([P, 2, A], U8, name="raw_scales_q", align_bytes=64)
        nc.vector.memset(raw_scales["q"][:].bitcast(I32), 0)

        ident = keep.tile([P, P], F32, name="ident")
        make_identity(nc, ident[:])

        directions = {}
        raw_words = {}
        tokens = {}

        def load_directions(side, n):
            source = dq if side == "q" else dk
            both = keep.tile([P, 2, D], BF16, name="dir_%s%d" % (side, n), align_bytes=64)
            nc.sync.dma_start(out=both[:], in_=source[PAIR * n : PAIR * (n + 1), :].rearrange("(s p) d -> p s d", p=P))
            for s in range(2):
                directions[side, n, s] = both[:, s, :]

        def load_weight_words(side):
            source = wq_words if side == "q" else wk_words
            raw_words[side] = keep.tile([P, 2, 2 * A], U8, name="raw_words_" + side, align_bytes=64)
            nc.sync.dma_start(out=raw_words[side][:].bitcast(I32), in_=source.rearrange("g p n -> p g n").bitcast(I32))

        def load_weight_scales(side):
            source = wq_scales if side == "q" else wk_scales
            for quad in range(4):
                nc.sync.dma_start(
                    out=raw_scales[side][QUADRANT * quad : QUADRANT * quad + 4, :, :].bitcast(I32),
                    in_=source[:, 4 * quad : 4 * quad + 4, :].rearrange("g r n -> r g n").bitcast(I32),
                )

        def load_tokens(side, half):
            source = aq if side == "q" else ak
            tokens[side, half] = keep.tile([P, 4, HALF], BF16, name="tok_%s%d" % (side, half), align_bytes=64)
            nc.sync.dma_start(
                out=tokens[side, half][:],
                in_=source[:, HALF * half : HALF * (half + 1)].rearrange("(p t) n -> p t n", t=4),
            )

        for s in range(2):
            single = keep.tile([P, D], BF16, name="dir_k0_%d" % s, align_bytes=64)
            nc.sync.dma_start(out=single[:], in_=dk[P * s : P * (s + 1), :])
            directions["k", 0, s] = single[:]
        load_weight_scales("k")
        load_weight_words("k")
        load_directions("k", 1)
        nc.sync.dma_start(out=g_rows[:], in_=g.rearrange("(p t) -> p t", t=4))
        load_tokens("k", 0)
        load_directions("q", 0)
        load_weight_words("q")
        load_weight_scales("q")
        load_tokens("q", 0)
        load_directions("k", 2)
        load_tokens("k", 1)
        load_directions("k", 3)
        load_tokens("q", 1)
        for n in range(1, 4):
            load_directions("q", n)

        weights = {}
        turned = {}
        dir_mx = {}
        projected = {}
        proj_mx = {("k", half): operand("k%d" % half, HALF) for half in range(2)}
        for n in range(4):
            proj_mx["q", n] = operand("q%d" % n, PAIR)
        tok_mx = {(side, half): operand("a%s%d" % (side, half), HALF) for side in ("q", "k") for half in range(2)}
        tok_grouped = {}
        coact = {}
        results = {}
        rounded = {}
        plane_in = {}
        plane_codes = keep.tile([P, 2, F], U32, name="plane_codes", align_bytes=256)
        plane_scales = keep.tile([P, F], U8, name="plane_scales", align_bytes=256)

        def sort_weight(side):
            words = keep.tile([P, 2, 2 * A], U8, name="words_" + side, align_bytes=256)
            scales = keep.tile([P, 2, A], U8, name="scales_" + side, align_bytes=256)
            for target, source in ((words, raw_words[side]), (scales, raw_scales[side])):
                nc.vector.tensor_copy(
                    out=target[:].bitcast(I32).rearrange("p g (t b w) -> p g t b w", t=4, b=16),
                    in_=source[:].bitcast(I32).rearrange("p g (b t w) -> p g t b w", t=4, b=16),
                )
            weights[side] = (words, scales)

        def turn(side, n, engines=SCALAR):
            turned[side, n] = flow.tile([P, 2 * D], BF16, name="turned_%s%d" % (side, n), tag="turned", align_bytes=64)
            for s in range(2):
                doubles = directions[side, n, s].bitcast(F32)
                bank = next_bank()
                for grp in range(2):
                    for u in range(2):
                        place = P * (2 * grp + u)
                        every_second = doubles[:, PAIR * grp + u : PAIR * (grp + 1) : 2]
                        nc.tensor.transpose(bank[:, place : place + P], every_second, ident[:])
                move(
                    engines[s],
                    turned[side, n][:, D * s : D * (s + 1)].bitcast(F32).rearrange("p (g f u) -> p g f u", g=2, u=2),
                    bank[:].rearrange("p (g u f) -> p g f u", g=2, u=2),
                )

        def quantize_turned(side, n, pieces=1):
            codes = flow.tile([P, HALF], U32, name="dir_codes_%s%d" % (side, n), tag="dir_codes", align_bytes=256)
            scales = flow.tile([P, HALF], U8, name="dir_scales_%s%d" % (side, n), tag="dir_scales", align_bytes=256)
            dir_mx[side, n] = (codes, scales)
            width = HALF // pieces
            for piece in range(pieces):
                cols = slice(width * piece, width * (piece + 1))
                quantize(dir_mx[side, n], cols, turned[side, n][:, 4 * cols.start : 4 * cols.stop])

        def project(side, n):
            words, word_scales = weights[side]
            codes, scales = dir_mx[side, n]
            projected[side, n] = flow.tile([P, 4 * PAIR], BF16, name="proj_%s%d" % (side, n), tag="proj", align_bytes=64)
            for s in range(2):
                bank = next_bank()
                for t in range(4):
                    for grp in range(2):
                        cols = slice(P * (2 * s + grp), P * (2 * s + grp + 1))
                        nc.tensor.matmul_mx(
                            out=bank[:, P * t : P * (t + 1)],
                            lhsT=words[:, grp, 2 * P * t : 2 * P * (t + 1)].bitcast(FP4X4),
                            lhsT_scale=word_scales[:, grp, P * t : P * (t + 1)],
                            rhs=codes[:, cols].bitcast(FP8X4),
                            rhs_scale=scales[:, cols],
                            start=(grp == 0),
                            stop=(grp == 1),
                        )
                target = projected[side, n][:, HALF * s : HALF * (s + 1)].rearrange("p (f t) -> p f t", t=4)
                source = bank[:].rearrange("p (t f) -> p f t", t=4)
                if side == "q":
                    nc.scalar.activation(out=target, in_=source, func=COPY, scale=head_col[:])
                else:
                    nc.scalar.copy(out=target, in_=source)

        def quantize_projected(side, n):
            if side == "q":
                quantize(proj_mx["q", n], slice(0, PAIR), projected[side, n][:])
            else:
                quantize(proj_mx["k", n // 2], slice(PAIR * (n % 2), PAIR * (n % 2 + 1)), projected[side, n][:])

        def weigh_tokens(half):
            weighed = flow.tile([P, 4, HALF], BF16, name="weighed%d" % half, tag="weighed", align_bytes=64)
            for t in range(4):
                nc.vector.tensor_scalar(
                    out=weighed[:, t, :], in0=tokens["k", half][:, t, :], scalar1=g_rows[:, t : t + 1], scalar2=None, op0=MULT
                )
            tokens["k", half] = weighed

        def group_tokens(side, half):
            tok_grouped[side, half] = flow.tile(
                [P, 4 * HALF], BF16, name="grouped_%s%d" % (side, half), tag="grouped", align_bytes=64
            )
            nc.vector.tensor_copy(
                out=tok_grouped[side, half][:].rearrange("p (c i t) -> p c t i", i=4, t=4),
                in_=tokens[side, half][:].rearrange("p t (c i) -> p c t i", i=4),
            )

        def quantize_tokens(side, half):
            quantize(tok_mx[side, half], slice(0, HALF), tok_grouped[side, half][:])

        def coactivate(n, half):
            coact[n, half] = flow.tile([P, 2, HALF], F32, name="coact%d_%d" % (n, half), tag="coact", bufs=5)
            for s in range(2):
                bank = next_bank()
                product(bank[:], tok_mx["q", n // 2], PAIR * (n % 2) + P * s, tok_mx["k", half])
                nc.scalar.copy(out=coact[n, half][:, s, :], in_=bank[:])

        def score(n, half):
            results[n, half] = flow.tile([P, 2, HALF], F32, name="result%d_%d" % (n, half), tag="result", bufs=4)
            for s in range(2):
                bank = next_bank()
                product(bank[:], proj_mx["q", n], P * s, proj_mx["k", half])
                nc.vector.scalar_tensor_tensor(
                    out=results[n, half][:, s, :],
                    in0=bank[:],
                    scalar=OUT_FACTOR,
                    in1=coact[n, half][:, s, :],
                    op0=MULT,
                    op1=MULT,
                )
            nc.sync.dma_start(
                out=out_0[PAIR * n : PAIR * (n + 1), HALF * half : HALF * (half + 1)].rearrange("(s p) j -> p s j", p=P),
                in_=results[n, half][:],
            )

        def rounded_tile(n, half):
            rounded[n, half] = flow.tile(
                [P, 2 * HALF], BF16, name="rounded%d_%d" % (n, half), tag="rounded", bufs=6, align_bytes=64
            )
            return rounded[n, half]

        def round_result(n, half):
            nc.vector.tensor_copy(
                out=rounded_tile(n, half)[:].rearrange("f (s u p e) -> f s u p e", s=2, u=2, e=2),
                in_=results[n, half][:].rearrange("f s (p u e) -> f s u p e", u=2, e=2),
            )

        def round_result_by_tile(n, half, engines):
            target = rounded_tile(n, half)
            for s in range(2):
                move(
                    engines[s],
                    target[:, HALF * s : HALF * (s + 1)].rearrange("f (u p e) -> f u p e", u=2, e=2),
                    results[n, half][:, s, :].rearrange("f (p u e) -> f u p e", u=2, e=2),
                )

        def turn_result(n, half):
            doubles = rounded[n, half][:].bitcast(F32)
            bank = next_bank()
            for place in range(0, HALF, P):
                nc.tensor.transpose(bank[:, place : place + P], doubles[:, place : place + P], ident[:])
            plane_in[n, half] = flow.tile(
                [P, 4 * PAIR], BF16, name="plane_in%d_%d" % (n, half), tag="plane_in", bufs=8, align_bytes=64
            )
            nc.scalar.copy(
                out=plane_in[n, half][:].bitcast(F32).rearrange("p (s f u) -> p s f u", s=2, u=2),
                in_=bank[:].rearrange("p (s u f) -> p s f u", s=2, u=2),
            )

        def quantize_result(n, half):
            cols = slice(PAIR * n, PAIR * (n + 1))
            nc.vector.quantize_mx(
                out=plane_codes[:, half, cols].bitcast(FP8X4),
                scales=plane_scales[4 * half : P, cols],
                in_=plane_in[n, half][:],
            )
            nc.sync.dma_start(
                out=out_1[half, :, cols, :].rearrange("p f t -> p (f t)").bitcast(I32),
                in_=plane_codes[:, half, cols].bitcast(I32),
            )

        sort_weight("k")
        turn("k", 0, SHARED)
        quantize_turned("k", 0, pieces=2)

        turn("k", 1)
        project("k", 0)
        weigh_tokens(0)
        group_tokens("k", 0)
        quantize_turned("k", 1)

        turn("q", 0)
        project("k", 1)
        sort_weight("q")
        quantize_tokens("k", 0)
        quantize_turned("q", 0)
        group_tokens("q", 0)
        quantize_projected("k", 0)

        turn("k", 2)
        project("q", 0)
        quantize_tokens("q", 0)
        quantize_projected("k", 1)
        quantize_turned("k", 2)
        coactivate(0, 0)
        weigh_tokens(1)
        quantize_projected("q", 0)
        group_tokens("k", 1)

        turn("k", 3)
        score(0, 0)
        project("k", 2)
        coactivate(1, 0)
        quantize_turned("k", 3)
        quantize_tokens("k", 1)
        group_tokens("q", 1)

        turn("q", 1)
        project("k", 3)
        coactivate(0, 1)
        quantize_projected("k", 2)
        round_result(0, 0)
        quantize_turned("q", 1)
        quantize_projected("k", 3)
        quantize_tokens("q", 1)

        turn("q", 2, SHARED)
        turn_result(0, 0)
        score(0, 1)
        project("q", 1)
        coactivate(1, 1)
        quantize_turned("q", 2)
        round_result(0, 1)
        quantize_projected("q", 1)
        quantize_result(0, 0)

        turn("q", 3, SHARED)
        turn_result(0, 1)
        score(1, 0)
        coactivate(2, 0)
        quantize_turned("q", 3)
        score(1, 1)
        project("q", 2)
        round_result(1, 0)
        quantize_result(0, 1)
        project("q", 3)
        quantize_projected("q", 2)
        round_result(1, 1)
        coactivate(2, 1)
        quantize_projected("q", 3)

        for half in range(2):
            score(2, half)
            round_result_by_tile(2, half, GPSIMD)
            coactivate(3, half)
        score(3, 0)
        score(3, 1)
        round_result_by_tile(3, 0, SHARED)

        turn_result(1, 0)
        turn_result(1, 1)
        turn_result(2, 0)
        turn_result(2, 1)
        round_result(3, 1)
        turn_result(3, 0)
        quantize_result(1, 0)
        turn_result(3, 1)
        for n, half in ((2, 0), (1, 1), (3, 0), (2, 1), (3, 1)):
            quantize_result(n, half)

        for quad in range(4):
            nc.scalar.dma_start(
                out=out_2[:, 4 * quad : 4 * quad + 4, :].bitcast(I32),
                in_=plane_scales[QUADRANT * quad : QUADRANT * quad + 8, :].bitcast(I32),
            )
